import numpy as np
import ml_dtypes


def mxq(x, axis, fmt="e4m3"):
    dtype, down = {"e4m3": (ml_dtypes.float8_e4m3fn, 7), "e5m2": (ml_dtypes.float8_e5m2, 14)}[fmt]
    v = np.moveaxis(np.asarray(x, np.float32).astype(ml_dtypes.bfloat16).astype(np.float64), axis, -1)
    blocks = v.reshape(v.shape[:-1] + (-1, 32))
    amax = np.abs(blocks).max(-1, keepdims=True)
    byte = np.maximum(np.where(amax > 0, np.frexp(amax)[1] - 1 + 127, 0) - down, 1)
    scale = np.exp2(byte - 127.0)
    codes = (blocks / scale).astype(np.float32).astype(dtype).astype(np.float64)
    return np.moveaxis((codes * scale).reshape(v.shape), -1, axis)


WIDE = False


def mx_kscale(k):
    if not WIDE:
        return np.ones(k)
    levels = np.array([10, -10, 5, -5, 0])
    if k % 512:
        return np.exp2(np.random.permutation(np.resize(levels, k // 32))).repeat(32)
    a = np.empty((k // 512, 16))
    for p in range(k // 512):
        a[p, :8] = np.random.permutation(np.resize(levels, 8))
        for g in range(8):
            far = levels[np.abs(levels - a[p, g]) >= 10]
            a[p, g + 8] = far[np.random.randint(len(far))]
    return np.exp2(a.ravel()).repeat(32)


BF16 = ml_dtypes.bfloat16


def bf(x):
    return np.asarray(x, np.float32).astype(BF16)


def f64(x):
    return np.asarray(x).astype(np.float64)


E2M1 = np.array([0.0, 0.5, 1.0, 1.5, 2.0, 3.0, 4.0, 6.0, -0.0, -0.5, -1.0, -1.5, -2.0, -3.0, -4.0, -6.0])


def pack_weight(w, fmt):
    k, n = w.shape
    w = f64(bf(w)).reshape(k // 32, 32, n)
    amax = np.abs(w).max(1)
    if fmt == "e4m3":
        byte = np.frexp(amax)[1] - 1 + 127 - 7
    else:
        mant, ex = np.frexp(amax / 6.0)
        byte = np.where(mant > 0.5, ex, ex - 1) + 127
    byte = np.clip(np.where(amax > 0, byte, 1), 1, 254)
    scaled = (w * np.exp2(127.0 - byte)[:, None, :]).reshape(k, n).astype(np.float32)
    by_word = np.ascontiguousarray(scaled.reshape(k // 512, 128, 4, n).transpose(0, 1, 3, 2))
    if fmt == "e4m3":
        words = by_word.astype(ml_dtypes.float8_e4m3fn).view(np.uint8)
    else:
        c = by_word.astype(ml_dtypes.float4_e2m1fn).view(np.uint8) & 0xF
        words = c[..., 0::2] | (c[..., 1::2] << 4)
    return np.ascontiguousarray(words), np.ascontiguousarray(byte.astype(np.uint8).reshape(k // 512, 16, n))


def unpack_weight(words, scales, fmt):
    g, p, n, _ = words.shape
    if fmt == "e4m3":
        vals = np.ascontiguousarray(words).view(ml_dtypes.float8_e4m3fn).astype(np.float64)
    else:
        nib = np.empty((g, p, n, 4), np.uint8)
        nib[..., 0::2] = words & 0xF
        nib[..., 1::2] = words >> 4
        vals = E2M1[nib]
    vals = vals * np.repeat(np.exp2(scales.astype(np.float64) - 127.0), 8, axis=1)[..., None]
    return vals.transpose(0, 1, 3, 2).reshape(g * 512, n)
def pack4(w):
    words, scales = pack_weight(w, "e2m1")
    return words.reshape(words.shape[0], 128, -1), scales


def unpack4(words, scales):
    return unpack_weight(words.reshape(words.shape[0], 128, -1, 2), scales, "e2m1")


def planes(Y):
    n, m = Y.shape
    b = f64(bf(Y)).reshape(n // 32, 32, m)
    amax = np.abs(b).max(1)
    byte = np.clip(np.where(amax > 0, np.frexp(amax)[1] - 1 + 127 - 7, 1), 1, 254)
    codes = (b * np.exp2(127.0 - byte)[:, None, :]).reshape(n, m).astype(np.float32).astype(ml_dtypes.float8_e4m3fn).view(np.uint8)
    words = codes.reshape(n // 512, 128, 4, m).transpose(0, 1, 3, 2)
    return np.ascontiguousarray(words), np.ascontiguousarray(byte.astype(np.uint8).reshape(n // 512, 16, m))


T, D, F = 1024, 1024, 2048


def tanh_penalty_slope(h, lam):
    th = np.tanh(h)
    return lam[None, :] * (1.0 - th * th)


def setup_inputs():
    s, u = mx_kscale(D), mx_kscale(T)
    x = bf(np.random.standard_normal((T, D)) / u[:, None])
    h = bf(np.random.standard_normal((T, F)))
    r = bf(np.random.standard_normal((T, D)) * s)
    wdec = np.random.standard_normal((F, D)) / np.sqrt(D) / s
    wdec_words, wdec_scales = pack4(wdec.T)
    return {"x": x,
            "h": h,
            "r": r,
            "wdec_words": wdec_words,
            "wdec_scales": wdec_scales,
            "lam": bf(np.random.uniform(0.5, 1.5, F)),
            "w": bf((1.0 + 0.1 * np.random.standard_normal(T)) * u)}


def core(x, h, r, wdec_words, wdec_scales, lam, w):
    x, h, r, lam, w = f64(x), f64(h), f64(r), f64(lam), f64(w)
    tokens = x.shape[0]
    up = mxq(r, 1, "e4m3") @ unpack4(wdec_words, wdec_scales)
    pen = tanh_penalty_slope(h, lam)
    g = np.where(h > 0, up + pen, 0.0)
    g = g * w[:, None]
    return (mxq(x, 0, "e4m3").T @ mxq(g, 0, "e4m3")) / np.sqrt(tokens)


def reference(x, h, r, wdec_words, wdec_scales, lam, w):
    R_out = core(x, h, r, wdec_words, wdec_scales, lam, w)
    words, scales = planes(R_out)
    return R_out, words, scales

@@ -1,0 +1,381 @@
+from contextlib import ExitStack
+
+import concourse.mybir as mybir
+from concourse.masks import make_identity
+
+T, D, F = 1024, 1024, 2048
+FLOPS = 2 * (2 * T * D * F)
+BYTES = 2 * (T * D + T * F + T * D + F + T) + D * F // 2 + D * F // 32 + 4 * D * F + D * F + D * F // 32
+
+P = 128
+WID = [256,512,512,512,256]
+OFF = [sum(WID[:i]) for i in range(len(WID))]
+NK = len(WID)
+UNITS = 2 * NK
+CG = [256,256,480,480,480,480,480,480,0,0]
+VC = [0,0,128,0,0,0,256,128]
+
+F32 = mybir.dt.float32
+BF16 = mybir.dt.bfloat16
+U32 = mybir.dt.uint32
+I32 = mybir.dt.int32
+U8 = mybir.dt.uint8
+E4M3 = mybir.dt.float8_e4m3fn_x4
+E2M1 = mybir.dt.float4_e2m1fn_x4
+ALU = mybir.AluOpType
+ACT = mybir.ActivationFunctionType
+
+
+def tile_transcodertanhpenaltyencodervjp_x2_kernel(tc, x, h, r, wdec_words, wdec_scales, lam, w, out_0, out_1, out_2):
+    nc = tc.nc
+    with ExitStack() as ctx:
+        const = ctx.enter_context(tc.tile_pool(name="const", bufs=1))
+        raws = ctx.enter_context(tc.tile_pool(name="raws", bufs=3))
+        hpool = ctx.enter_context(tc.tile_pool(name="hpool", bufs=8))
+        mpool = ctx.enter_context(tc.tile_pool(name="mpool", bufs=3))
+        thpool = ctx.enter_context(tc.tile_pool(name="thpool", bufs=4))
+        penpool = ctx.enter_context(tc.tile_pool(name="penpool", bufs=3))
+        ilpool = ctx.enter_context(tc.tile_pool(name="ilpool", bufs=5))
+        gqpool = ctx.enter_context(tc.tile_pool(name="gqpool", bufs=4))
+        ypool = ctx.enter_context(tc.tile_pool(name="ypool", bufs=3))
+        up_ps = ctx.enter_context(tc.psum_pool(name="up_ps", bufs=4))
+        y_ps = ctx.enter_context(tc.psum_pool(name="y_ps", bufs=3))
+        lam_ps = ctx.enter_context(tc.psum_pool(name="lam_ps", bufs=1))
+
+        ident = const.tile([P, P], F32, name="ident")
+        w_raw = const.tile([P, 2, 4], BF16, name="w_raw")
+        w_col = const.tile([P, 2, 4], F32, name="w_col")
+        lam_rows = const.tile([P, P], BF16, name="lam_rows")
+        lam_f32 = const.tile([P, P], F32, name="lam_f32")
+        lam_cols = const.tile([P, 16], F32, name="lam_cols")
+        w_words = [const.tile([P, 2, 2 * WID[k]], U8, name="w_words%d" % k, align_bytes=64) for k in range(NK)]
+        w_scales = const.tile([P, 2, F], U8, name="w_scales", align_bytes=64)
+        rq = [[const.tile([P, 512], U32, name="rq%d%d" % (g, c), align_bytes=64) for c in range(2)] for g in range(2)]
+        rs = [[const.tile([P, 512], U8, name="rs%d%d" % (g, c), align_bytes=64) for c in range(2)] for g in range(2)]
+        xq = [[const.tile([P, 512], U32, name="xq%d%d" % (g, c), align_bytes=64) for c in range(2)] for g in range(2)]
+        xs = [[const.tile([P, 512], U8, name="xs%d%d" % (g, c), align_bytes=64) for c in range(2)] for g in range(2)]
+        ys = const.tile([P, 2, OFF[-1]], U8, name="ys", align_bytes=64)
+        ys_end = const.tile([P, 2, WID[-1]], U8, name="ys_end", align_bytes=64)
+
+        ctx.enter_context(tc.manual_schedule())
+
+        h_t, m_t, th_t, pen_t, g_t, gq_t, gs_t = {}, {}, {}, {}, {}, {}, {}
+        up_t, y32_t, yil_t, yb_t = {}, {}, {}, {}
+        r_raw, x_raw, rg_t, rb_t = {}, {}, {}, {}
+
+        def load_h(u):
+            k, g = divmod(u, 2)
+            h_t[u] = hpool.tile([P, 4, WID[k]], BF16, name="h_in")
+            src = h[512 * g : 512 * g + 512, OFF[k] : OFF[k] + WID[k]].rearrange("(p t) f -> p t f", t=4)
+            nc.sync.dma_start(out=h_t[u][:], in_=src)
+
+        def load_rows(dst, src, g, lo=0, hi=4):
+            if lo == 0:
+                dst[g] = raws.tile([P, 4, D], BF16, name="raw")
+            rows = src[512 * g : 512 * g + 512, :].rearrange("(p t) d -> p t d", t=4)
+            nc.sync.dma_start(out=dst[g][:, lo:hi, :], in_=rows[:, lo:hi, :])
+
+        def load_words(k):
+            cols = slice(2 * OFF[k], 2 * (OFF[k] + WID[k]))
+            nc.sync.dma_start(out=w_words[k][:].bitcast(I32), in_=wdec_words[:, :, cols].rearrange("c p b -> p c b").bitcast(I32))
+
+        def load_w_scales():
+            for q in range(4):
+                nc.sync.dma_start(
+                    out=w_scales[32 * q : 32 * q + 4, :, :].bitcast(I32), in_=wdec_scales[:, 4 * q : 4 * q + 4, :].rearrange("c q n -> q c n").bitcast(I32)
+                )
+
+        def r_transposes(g, pool, nm):
+            for tp in range(2):
+                for c in range(2):
+                    bank = pool.tile([P, 512], F32, name=nm)
+                    rb_t[(g, c, tp)] = bank
+                    for t in range(2):
+                        words = r_raw[g][:, 2 * tp + t, :].bitcast(F32)
+                        for e in range(2):
+                            o = (2 * t + e) * P
+                            nc.tensor.transpose(bank[:, o : o + P], words[:, 256 * c + e : 256 * (c + 1) : 2], ident[:])
+
+        def copy(engine, out, in_):
+            if engine == "v":
+                nc.vector.tensor_copy(out=out, in_=in_)
+            else:
+                nc.scalar.copy(out=out, in_=in_)
+
+        def r_copy(g, c, tp, engine):
+            if tp == 0:
+                rg_t[(g, c)] = ilpool.tile([P, 2048], BF16, name="grouped", align_bytes=64)
+            dst = rg_t[(g, c)][:].bitcast(F32)[:, 512 * tp : 512 * (tp + 1)].rearrange("p (t m e) -> p t m e", t=2, e=2)
+            copy(engine, dst, rb_t[(g, c, tp)][:].rearrange("p (t e m) -> p t m e", t=2, e=2))
+
+        def r_quant(g, c):
+            nc.vector.quantize_mx(out=rq[g][c][:].bitcast(E4M3), scales=rs[g][c][:], in_=rg_t[(g, c)][:])
+
+        def x_copy(g, half, engine):
+            xg = ilpool.tile([P, 2048], BF16, name="grouped", align_bytes=64)
+            rg_t[("x", g, half)] = xg
+            dst = xg[:].rearrange("p (t m j) -> p t m j", t=4, j=4)
+            copy(engine, dst, x_raw[g][:, :, 512 * half : 512 * half + 512].rearrange("p j (m t) -> p t m j", t=4))
+
+        def x_quant(g, half):
+            nc.vector.quantize_mx(out=xq[g][half][:].bitcast(E4M3), scales=xs[g][half][:], in_=rg_t[("x", g, half)][:])
+
+        lam_bank = {}
+
+        def lam_transposes(k):
+            bank = lam_ps.tile([P, 512], F32, name="lam_bank")
+            lam_bank[k] = bank
+            for b in range(WID[k] // P):
+                col = OFF[k] // P + b
+                nc.tensor.transpose(bank[:, P * b : P * b + P], lam_cols[:, col : col + 1].to_broadcast([P, P]), ident[:])
+
+        def tanh(u):
+            th_t[u] = thpool.tile([P, 4, WID[u // 2]], F32, name="th")
+            nc.scalar.activation(out=th_t[u][:], in_=h_t[u][:], func=ACT.Tanh)
+
+        def square(u):
+            nc.scalar.activation(out=th_t[u][:], in_=th_t[u][:], func=ACT.Square)
+
+        def mask(u):
+            k, g = divmod(u, 2)
+            m_t[u] = mpool.tile([P, 4, WID[k]], BF16, name="mask")
+            for t in range(4):
+                nc.vector.tensor_scalar(out=m_t[u][:, t, :], in0=h_t[u][:, t, :], scalar1=0.0, scalar2=w_col[:, g, t : t + 1], op0=ALU.is_gt, op1=ALU.mult)
+
+        def step_a(u):
+            n = WID[u // 2]
+            pen_t[u] = penpool.tile([P, 4, n], F32, name="pen")
+            nc.vector.scalar_tensor_tensor(
+                out=pen_t[u][:], in0=th_t[u][:], scalar=1.0, in1=lam_bank[u // 2][:, 0:n].unsqueeze(1).to_broadcast([P, 4, n]), op0=ALU.subtract, op1=ALU.mult
+            )
+
+        def stage1(u):
+            k, g = divmod(u, 2)
+            n = 512 if WID[k] == 512 else 128
+            for t in range(4):
+                bank = up_ps.tile([P, 512], F32, name="up")
+                up_t[(u, t)] = bank
+                for lo in range(0, WID[k], n):
+                    for c in range(2):
+                        nc.tensor.matmul_mx(
+                            out=bank[:, lo : lo + n],
+                            lhsT=rq[g][c][:, P * t : P * t + P].bitcast(E4M3),
+                            lhsT_scale=rs[g][c][:, P * t : P * t + P],
+                            rhs=w_words[k][:, c, 2 * lo : 2 * (lo + n)].bitcast(E2M1),
+                            rhs_scale=w_scales[:, c, OFF[k] + lo : OFF[k] + lo + n],
+                            start=(c == 0),
+                            stop=(c == 1),
+                        )
+
+        def step_b(u):
+            for t in range(4):
+                nc.vector.tensor_tensor(out=pen_t[u][:, t, :], in0=up_t[(u, t)][:, 0 : WID[u // 2]], in1=pen_t[u][:, t, :], op=ALU.subtract)
+
+        def step_c(u, lo, hi, engine):
+            if hi <= lo:
+                return
+            if u not in g_t:
+                g_t[u] = ilpool.tile([P, 4 * WID[u // 2]], BF16, name="grouped", align_bytes=64)
+            args = dict(
+                out=g_t[u][:, 4 * lo : 4 * hi].rearrange("p (c i t) -> p c t i", i=4, t=4),
+                in0=pen_t[u][:, :, lo:hi].rearrange("p t (c i) -> p c t i", i=4),
+                in1=m_t[u][:, :, lo:hi].rearrange("p t (c i) -> p c t i", i=4),
+                op=ALU.mult,
+            )
+            if engine == "v":
+                nc.vector.tensor_tensor(**args)
+            else:
+                nc.gpsimd.tensor_tensor(**args)
+
+        def g_quant(u):
+            gq_t[u] = gqpool.tile([P, WID[u // 2]], U32, name="gq", align_bytes=64)
+            gs_t[u] = gqpool.tile([P, WID[u // 2]], U8, name="gs", align_bytes=64)
+            nc.vector.quantize_mx(out=gq_t[u][:].bitcast(E4M3), scales=gs_t[u][:], in_=g_t[u][:])
+
+        def stage2(k, half, pool, nm):
+            for t in range(4):
+                bank = pool.tile([P, 512], F32, name=nm)
+                yb_t[(k, half, t)] = bank
+                for g in range(2):
+                    u = 2 * k + g
+                    nc.tensor.matmul_mx(
+                        out=bank[:, 0 : WID[k]],
+                        lhsT=xq[g][half][:, P * t : P * t + P].bitcast(E4M3),
+                        lhsT_scale=xs[g][half][:, P * t : P * t + P],
+                        rhs=gq_t[u][:].bitcast(E4M3),
+                        rhs_scale=gs_t[u][:],
+                        start=(g == 0),
+                        stop=(g == 1),
+                    )
+
+        def y_out(k, half, t, engine):
+            if t == 0:
+                y32_t[(k, half)] = ypool.tile([P, 4, WID[k]], F32, name="y32")
+            dst = y32_t[(k, half)][:, t, :]
+            src = yb_t[(k, half, t)][:, 0 : WID[k]]
+            if engine == "v":
+                nc.vector.tensor_scalar(out=dst, in0=src, scalar1=0.03125, scalar2=None, op0=ALU.mult)
+            else:
+                nc.scalar.activation(out=dst, in_=src, func=ACT.Copy, scale=0.03125)
+
+        def y_store(k, half, lo=0, hi=4):
+            dst = out_0[512 * half : 512 * half + 512, OFF[k] : OFF[k] + WID[k]].rearrange("(p t) m -> p t m", t=4)
+            nc.sync.dma_start(out=dst[:, lo:hi, :], in_=y32_t[(k, half)][:, lo:hi, :])
+
+        def y_group(k, half, lo, hi, engine):
+            if hi <= lo:
+                return
+            if (k, half) not in yil_t:
+                yil_t[(k, half)] = ilpool.tile([P, 4 * WID[k]], BF16, name="grouped", align_bytes=64)
+            dst = yil_t[(k, half)][:, 4 * lo : 4 * hi].rearrange("p (c i t) -> p c t i", i=4, t=4)
+            copy(engine, dst, y32_t[(k, half)][:, :, lo:hi].rearrange("p t (c i) -> p c t i", i=4))
+
+        def y_quant(k, half):
+            yq = gqpool.tile([P, WID[k]], U32, name="yq", align_bytes=64)
+            cols = slice(OFF[k], OFF[k] + WID[k])
+            nc.vector.quantize_mx(out=yq[:].bitcast(E4M3), scales=ys_end[:, half, :] if k == NK - 1 else ys[:, half, cols], in_=yil_t[(k, half)][:])
+            nc.sync.dma_start(out=out_1[half, :, cols, :].rearrange("p m t -> p (m t)").bitcast(I32), in_=yq[:].bitcast(I32))
+
+        def y_scales(src, lo, hi):
+            for q in range(4):
+                nc.sync.dma_start(
+                    out=out_2[:, 4 * q : 4 * q + 4, lo:hi].rearrange("c q n -> q c n").bitcast(I32), in_=src[32 * q : 32 * q + 4, :, :].bitcast(I32)
+                )
+
+        make_identity(nc, ident[:])
+        nc.gpsimd.memset(w_scales[:].rearrange("p c n -> p (c n)").bitcast(I32), 0)
+        nc.vector.memset(lam_rows[:], 0.0)
+        load_h(0)
+        load_rows(r_raw, r, 0, 0, 2)
+        load_rows(r_raw, r, 0, 2, 4)
+        nc.sync.dma_start(out=w_raw[:], in_=w.rearrange("(g p t) -> p g t", p=P, t=4))
+        nc.sync.dma_start(out=lam_rows[0:16, :], in_=lam.rearrange("(k p) -> k p", p=P))
+        load_words(0)
+        load_w_scales()
+        load_h(1)
+        load_rows(r_raw, r, 1)
+        load_h(2)
+        load_rows(x_raw, x, 0)
+        load_h(3)
+        load_rows(x_raw, x, 1)
+        load_words(1)
+        for u in range(4, UNITS):
+            load_h(u)
+            if u % 2 == 1:
+                load_words(u // 2)
+
+        tanh(0)
+        square(0)
+        r_transposes(0, up_ps, "up")
+        r_copy(0, 0, 0, "v")
+        r_copy(0, 1, 0, "s")
+        r_copy(0, 0, 1, "v")
+        r_copy(0, 1, 1, "v")
+        tanh(1)
+        square(1)
+        nc.vector.tensor_copy(out=lam_f32[:], in_=lam_rows[:])
+        nc.vector.tensor_copy(out=w_col[:], in_=w_raw[:])
+        lamT = lam_ps.tile([P, 512], F32, name="lam_bank")
+        nc.tensor.transpose(lamT[:, 0:P], lam_f32[:], ident[:])
+        r_quant(0, 0)
+        r_quant(0, 1)
+        nc.vector.tensor_copy(out=lam_cols[:], in_=lamT[:, 0:16])
+        lam_transposes(0)
+        stage1(0)
+        mask(0)
+        r_transposes(1, y_ps, "yb")
+        step_a(0)
+        tanh(2)
+
+        for u in range(UNITS):
+            last = u == UNITS - 1
+            ku, hu = divmod(u - 3, 2)
+            if u == 0:
+                step_a(1)
+                step_b(0)
+                r_copy(1, 0, 0, "v")
+                r_copy(1, 1, 0, "v")
+                r_copy(1, 0, 1, "v")
+                r_copy(1, 1, 1, "v")
+                r_quant(1, 0)
+                r_quant(1, 1)
+            else:
+                if u + 1 < UNITS:
+                    step_a(u + 1)
+                step_b(u)
+            if u + 1 < UNITS:
+                stage1(u + 1)
+            if u % 2 == 0 and u + 2 < UNITS:
+                lam_transposes(u // 2 + 1)
+            if u + 2 < UNITS:
+                square(u + 2)
+            if u >= 3:
+                y_out(ku, hu, 0, "s")
+                y_out(ku, hu, 1, "s")
+            if u + 3 < UNITS:
+                tanh(u + 3)
+            if u >= 3:
+                y_out(ku, hu, 2, "s")
+                y_out(ku, hu, 3, "s")
+                y_store(ku, hu)
+            if u < 2:
+                x_copy(u, 0, "vvvs"[2 * u])
+                x_copy(u, 1, "vvvs"[2 * u + 1])
+            if u >= 1:
+                step_c(u - 1, CG[u - 1], WID[(u - 1) // 2], "v")
+            if u < 2:
+                x_quant(u, 0)
+                x_quant(u, 1)
+            if u >= 1:
+                g_quant(u - 1)
+            if last:
+                break
+            if u >= 4:
+                kp, hp = divmod(u - 4, 2)
+                y_quant(kp, hp)
+            if u >= 3:
+                y_group(ku, hu, 0, VC[u - 3], "v")
+                y_group(ku, hu, VC[u - 3], WID[ku], "s")
+            if u >= 2:
+                k2, h2 = divmod(u - 2, 2)
+                stage2(k2, h2, y_ps, "yb")
+            if u >= 1:
+                mask(u)
+            if u == UNITS - 2:
+                mask(u + 1)
+            step_c(u, 0, CG[u], "g")
+
+        z = NK - 1
+        n = WID[z]
+        m = 160
+        step_c(UNITS - 1, 0, n, "v")
+        y_quant(z - 2, 1)
+        g_quant(UNITS - 1)
+        y_group(z - 1, 0, 0, VC[UNITS - 4], "v")
+        y_group(z - 1, 0, VC[UNITS - 4], WID[z - 1], "s")
+        stage2(z - 1, 1, y_ps, "yb")
+        for t in range(4):
+            y_out(z - 1, 1, t, "s")
+        y_store(z - 1, 1)
+        stage2(z, 0, up_ps, "up")
+        y_quant(z - 1, 0)
+        stage2(z, 1, y_ps, "yb")
+        for t in range(4):
+            y_out(z, 0, t, "v" if t < 3 else "s")
+        y_store(z, 0)
+        y_group(z - 1, 1, 0, VC[UNITS - 3], "v")
+        y_group(z - 1, 1, VC[UNITS - 3], WID[z - 1], "s")
+        y_group(z, 0, 0, m, "v")
+        y_quant(z - 1, 1)
+        y_scales(ys, 0, OFF[z])
+        y_group(z, 0, m, n, "s")
+        y_out(z, 1, 0, "v")
+        y_out(z, 1, 1, "s")
+        y_quant(z, 0)
+        y_out(z, 1, 2, "s")
+        y_out(z, 1, 3, "v")
+        y_store(z, 1)
+        y_group(z, 1, m, n, "s")
+        y_group(z, 1, 0, m, "v")
+        y_quant(z, 1)
+        y_scales(ys_end, OFF[z], F)

@@ -12,8 +12,8 @@ WID = [256,512,512,512,256]
 OFF = [sum(WID[:i]) for i in range(len(WID))]
 NK = len(WID)
 UNITS = 2 * NK
-CG = [256,256,480,480,480,480,480,480,0,0]
-VC = [0,0,128,0,0,0,256,128]
+CG = [160,160,384,384,384,384,256,192,0,0]
+VC = [0,0,0,0,0,0,256,128]
 
 F32 = mybir.dt.float32
 BF16 = mybir.dt.bfloat16
@@ -54,8 +54,8 @@ def tile_transcodertanhpenaltyencodervjp_x2_kernel(tc, x, h, r, wdec_words, wdec
         rs = [[const.tile([P, 512], U8, name="rs%d%d" % (g, c), align_bytes=64) for c in range(2)] for g in range(2)]
         xq = [[const.tile([P, 512], U32, name="xq%d%d" % (g, c), align_bytes=64) for c in range(2)] for g in range(2)]
         xs = [[const.tile([P, 512], U8, name="xs%d%d" % (g, c), align_bytes=64) for c in range(2)] for g in range(2)]
-        ys = const.tile([P, 2, OFF[-1]], U8, name="ys", align_bytes=64)
-        ys_end = const.tile([P, 2, WID[-1]], U8, name="ys_end", align_bytes=64)
+        ys_cols = [(0, OFF[-2]), (OFF[-2], OFF[-1]), (OFF[-1], F)]
+        ys = [const.tile([P, 2, hi - lo], U8, name="ys%d" % i, align_bytes=64) for i, (lo, hi) in enumerate(ys_cols)]
 
         ctx.enter_context(tc.manual_schedule())
 
@@ -99,6 +99,8 @@ def tile_transcodertanhpenaltyencodervjp_x2_kernel(tc, x, h, r, wdec_words, wdec
         def copy(engine, out, in_):
             if engine == "v":
                 nc.vector.tensor_copy(out=out, in_=in_)
+            elif engine == "g":
+                nc.gpsimd.tensor_scalar(out=out, in0=in_, scalar1=1.0, scalar2=1.0, op0=ALU.mult, op1=ALU.mult)
             else:
                 nc.scalar.copy(out=out, in_=in_)
 
@@ -112,6 +114,8 @@ def tile_transcodertanhpenaltyencodervjp_x2_kernel(tc, x, h, r, wdec_words, wdec
             nc.vector.quantize_mx(out=rq[g][c][:].bitcast(E4M3), scales=rs[g][c][:], in_=rg_t[(g, c)][:])
 
         def x_copy(g, half, engine):
+            if engine == "-":
+                return
             xg = ilpool.tile([P, 2048], BF16, name="grouped", align_bytes=64)
             rg_t[("x", g, half)] = xg
             dst = xg[:].rearrange("p (t m j) -> p t m j", t=4, j=4)
@@ -176,16 +180,18 @@ def tile_transcodertanhpenaltyencodervjp_x2_kernel(tc, x, h, r, wdec_words, wdec
                 return
             if u not in g_t:
                 g_t[u] = ilpool.tile([P, 4 * WID[u // 2]], BF16, name="grouped", align_bytes=64)
-            args = dict(
-                out=g_t[u][:, 4 * lo : 4 * hi].rearrange("p (c i t) -> p c t i", i=4, t=4),
-                in0=pen_t[u][:, :, lo:hi].rearrange("p t (c i) -> p c t i", i=4),
-                in1=m_t[u][:, :, lo:hi].rearrange("p t (c i) -> p c t i", i=4),
-                op=ALU.mult,
-            )
+            dst, a, b = g_t[u][:, 4 * lo : 4 * hi], pen_t[u][:, :, lo:hi], m_t[u][:, :, lo:hi]
             if engine == "v":
-                nc.vector.tensor_tensor(**args)
+                nc.vector.tensor_tensor(
+                    out=dst.rearrange("p (c i t) -> p c t i", i=4, t=4),
+                    in0=a.rearrange("p t (c i) -> p c t i", i=4),
+                    in1=b.rearrange("p t (c i) -> p c t i", i=4),
+                    op=ALU.mult,
+                )
             else:
-                nc.gpsimd.tensor_tensor(**args)
+                nc.gpsimd.tensor_tensor(
+                    out=dst.rearrange("p (n t) -> p n t", t=4), in0=a.rearrange("p t n -> p n t"), in1=b.rearrange("p t n -> p n t"), op=ALU.mult
+                )
 
         def g_quant(u):
             gq_t[u] = gqpool.tile([P, WID[u // 2]], U32, name="gq", align_bytes=64)
@@ -233,13 +239,16 @@ def tile_transcodertanhpenaltyencodervjp_x2_kernel(tc, x, h, r, wdec_words, wdec
         def y_quant(k, half):
             yq = gqpool.tile([P, WID[k]], U32, name="yq", align_bytes=64)
             cols = slice(OFF[k], OFF[k] + WID[k])
-            nc.vector.quantize_mx(out=yq[:].bitcast(E4M3), scales=ys_end[:, half, :] if k == NK - 1 else ys[:, half, cols], in_=yil_t[(k, half)][:])
+            i = max(0, k - NK + 3)
+            lo = OFF[k] - ys_cols[i][0]
+            nc.vector.quantize_mx(out=yq[:].bitcast(E4M3), scales=ys[i][:, half, lo : lo + WID[k]], in_=yil_t[(k, half)][:])
             nc.sync.dma_start(out=out_1[half, :, cols, :].rearrange("p m t -> p (m t)").bitcast(I32), in_=yq[:].bitcast(I32))
 
-        def y_scales(src, lo, hi):
+        def y_scales(i):
+            lo, hi = ys_cols[i]
             for q in range(4):
                 nc.sync.dma_start(
-                    out=out_2[:, 4 * q : 4 * q + 4, lo:hi].rearrange("c q n -> q c n").bitcast(I32), in_=src[32 * q : 32 * q + 4, :, :].bitcast(I32)
+                    out=out_2[:, 4 * q : 4 * q + 4, lo:hi].rearrange("c q n -> q c n").bitcast(I32), in_=ys[i][32 * q : 32 * q + 4, :, :].bitcast(I32)
                 )
 
         make_identity(nc, ident[:])
@@ -247,12 +256,12 @@ def tile_transcodertanhpenaltyencodervjp_x2_kernel(tc, x, h, r, wdec_words, wdec
         nc.vector.memset(lam_rows[:], 0.0)
         load_h(0)
         load_rows(r_raw, r, 0, 0, 2)
-        load_rows(r_raw, r, 0, 2, 4)
         nc.sync.dma_start(out=w_raw[:], in_=w.rearrange("(g p t) -> p g t", p=P, t=4))
         nc.sync.dma_start(out=lam_rows[0:16, :], in_=lam.rearrange("(k p) -> k p", p=P))
+        load_rows(r_raw, r, 0, 2, 4)
+        load_h(1)
         load_words(0)
         load_w_scales()
-        load_h(1)
         load_rows(r_raw, r, 1)
         load_h(2)
         load_rows(x_raw, x, 0)
@@ -267,14 +276,14 @@ def tile_transcodertanhpenaltyencodervjp_x2_kernel(tc, x, h, r, wdec_words, wdec
         tanh(0)
         square(0)
         r_transposes(0, up_ps, "up")
+        nc.vector.tensor_copy(out=w_col[:], in_=w_raw[:])
         r_copy(0, 0, 0, "v")
+        nc.vector.tensor_copy(out=lam_f32[:], in_=lam_rows[:])
         r_copy(0, 1, 0, "s")
         r_copy(0, 0, 1, "v")
         r_copy(0, 1, 1, "v")
         tanh(1)
         square(1)
-        nc.vector.tensor_copy(out=lam_f32[:], in_=lam_rows[:])
-        nc.vector.tensor_copy(out=w_col[:], in_=w_raw[:])
         lamT = lam_ps.tile([P, 512], F32, name="lam_bank")
         nc.tensor.transpose(lamT[:, 0:P], lam_f32[:], ident[:])
         r_quant(0, 0)
@@ -350,6 +359,7 @@ def tile_transcodertanhpenaltyencodervjp_x2_kernel(tc, x, h, r, wdec_words, wdec
         m = 160
         step_c(UNITS - 1, 0, n, "v")
         y_quant(z - 2, 1)
+        y_scales(0)
         g_quant(UNITS - 1)
         y_group(z - 1, 0, 0, VC[UNITS - 4], "v")
         y_group(z - 1, 0, VC[UNITS - 4], WID[z - 1], "s")
@@ -367,7 +377,7 @@ def tile_transcodertanhpenaltyencodervjp_x2_kernel(tc, x, h, r, wdec_words, wdec
         y_group(z - 1, 1, VC[UNITS - 3], WID[z - 1], "s")
         y_group(z, 0, 0, m, "v")
         y_quant(z - 1, 1)
-        y_scales(ys, 0, OFF[z])
+        y_scales(1)
         y_group(z, 0, m, n, "s")
         y_out(z, 1, 0, "v")
         y_out(z, 1, 1, "s")
@@ -378,4 +388,4 @@ def tile_transcodertanhpenaltyencodervjp_x2_kernel(tc, x, h, r, wdec_words, wdec
         y_group(z, 1, m, n, "s")
         y_group(z, 1, 0, m, "v")
         y_quant(z, 1)
-        y_scales(ys_end, OFF[z], F)
+        y_scales(2)

@@ -11,6 +11,7 @@ P = 128
 WID = [256,512,512,512,256]
 OFF = [sum(WID[:i]) for i in range(len(WID))]
 NK = len(WID)
+GI = 8
 UNITS = 2 * NK
 CG = [160,160,384,384,384,384,256,192,0,0]
 VC = [0,0,0,0,0,0,256,128]
@@ -190,7 +191,10 @@ def tile_transcodertanhpenaltyencodervjp_x2_kernel(tc, x, h, r, wdec_words, wdec
                 )
             else:
                 nc.gpsimd.tensor_tensor(
-                    out=dst.rearrange("p (n t) -> p n t", t=4), in0=a.rearrange("p t n -> p n t"), in1=b.rearrange("p t n -> p n t"), op=ALU.mult
+                    out=dst.rearrange("p (c i t) -> p c t i", i=GI, t=4),
+                    in0=a.rearrange("p t (c i) -> p c t i", i=GI),
+                    in1=b.rearrange("p t (c i) -> p c t i", i=GI),
+                    op=ALU.mult,
                 )
 
         def g_quant(u):

@@ -11,9 +11,9 @@ P = 128
 WID = [256,512,512,512,256]
 OFF = [sum(WID[:i]) for i in range(len(WID))]
 NK = len(WID)
-GI = 8
+GI = 4
 UNITS = 2 * NK
-CG = [160,160,384,384,384,384,256,192,0,0]
+CG = [160,160,384,384,384,384,320,192,0,0]
 VC = [0,0,0,0,0,0,256,128]
 
 F32 = mybir.dt.float32
@@ -174,7 +174,7 @@ def tile_transcodertanhpenaltyencodervjp_x2_kernel(tc, x, h, r, wdec_words, wdec
 
         def step_b(u):
             for t in range(4):
-                nc.vector.tensor_tensor(out=pen_t[u][:, t, :], in0=up_t[(u, t)][:, 0 : WID[u // 2]], in1=pen_t[u][:, t, :], op=ALU.subtract)
+                nc.vector.tensor_tensor(out=pen_t[u][:, t, :], in0=pen_t[u][:, t, :], in1=up_t[(u, t)][:, 0 : WID[u // 2]], op=ALU.add)
 
         def step_c(u, lo, hi, engine):
             if hi <= lo:
@@ -292,7 +292,7 @@ def tile_transcodertanhpenaltyencodervjp_x2_kernel(tc, x, h, r, wdec_words, wdec
         nc.tensor.transpose(lamT[:, 0:P], lam_f32[:], ident[:])
         r_quant(0, 0)
         r_quant(0, 1)
-        nc.vector.tensor_copy(out=lam_cols[:], in_=lamT[:, 0:16])
+        nc.vector.tensor_scalar(out=lam_cols[:], in0=lamT[:, 0:16], scalar1=-1.0, scalar2=None, op0=ALU.mult)
         lam_transposes(0)
         stage1(0)
         mask(0)

@@ -11,10 +11,13 @@ P = 128
 WID = [256,512,512,512,256]
 OFF = [sum(WID[:i]) for i in range(len(WID))]
 NK = len(WID)
+SPANS = [[0],[1,2],[3,4]]
+SPAN_OF = {k: s for s, ks in enumerate(SPANS) for k in ks}
+YO = ["ssss","ssss","ssss","ssss","ssss","ssss","ssss","ssss","ssss","ssss"]
 GI = 4
 UNITS = 2 * NK
-CG = [160,160,384,384,384,384,320,192,0,0]
-VC = [0,0,0,0,0,0,256,128]
+CG = [256,256,448,448,448,448,384,256,0,0]
+VC = [0,0,0,0,0,0,128,256]
 
 F32 = mybir.dt.float32
 BF16 = mybir.dt.bfloat16
@@ -32,11 +35,10 @@ def tile_transcodertanhpenaltyencodervjp_x2_kernel(tc, x, h, r, wdec_words, wdec
     with ExitStack() as ctx:
         const = ctx.enter_context(tc.tile_pool(name="const", bufs=1))
         raws = ctx.enter_context(tc.tile_pool(name="raws", bufs=3))
-        hpool = ctx.enter_context(tc.tile_pool(name="hpool", bufs=8))
-        mpool = ctx.enter_context(tc.tile_pool(name="mpool", bufs=3))
         thpool = ctx.enter_context(tc.tile_pool(name="thpool", bufs=4))
         penpool = ctx.enter_context(tc.tile_pool(name="penpool", bufs=3))
-        ilpool = ctx.enter_context(tc.tile_pool(name="ilpool", bufs=5))
+        ilpool = ctx.enter_context(tc.tile_pool(name="ilpool", bufs=3))
+        gpool = ctx.enter_context(tc.tile_pool(name="gpool", bufs=1))
         gqpool = ctx.enter_context(tc.tile_pool(name="gqpool", bufs=4))
         ypool = ctx.enter_context(tc.tile_pool(name="ypool", bufs=3))
         up_ps = ctx.enter_context(tc.psum_pool(name="up_ps", bufs=4))
@@ -51,24 +53,30 @@ def tile_transcodertanhpenaltyencodervjp_x2_kernel(tc, x, h, r, wdec_words, wdec
         lam_cols = const.tile([P, 16], F32, name="lam_cols")
         w_words = [const.tile([P, 2, 2 * WID[k]], U8, name="w_words%d" % k, align_bytes=64) for k in range(NK)]
         w_scales = const.tile([P, 2, F], U8, name="w_scales", align_bytes=64)
-        rq = [[const.tile([P, 512], U32, name="rq%d%d" % (g, c), align_bytes=64) for c in range(2)] for g in range(2)]
-        rs = [[const.tile([P, 512], U8, name="rs%d%d" % (g, c), align_bytes=64) for c in range(2)] for g in range(2)]
-        xq = [[const.tile([P, 512], U32, name="xq%d%d" % (g, c), align_bytes=64) for c in range(2)] for g in range(2)]
-        xs = [[const.tile([P, 512], U8, name="xs%d%d" % (g, c), align_bytes=64) for c in range(2)] for g in range(2)]
-        ys_cols = [(0, OFF[-2]), (OFF[-2], OFF[-1]), (OFF[-1], F)]
-        ys = [const.tile([P, 2, hi - lo], U8, name="ys%d" % i, align_bytes=64) for i, (lo, hi) in enumerate(ys_cols)]
+        rq = [const.tile([P, 2, 512], U32, name="rq%d" % g, align_bytes=64) for g in range(2)]
+        rs = [const.tile([P, 2, 512], U8, name="rs%d" % g, align_bytes=64) for g in range(2)]
+        xq = [const.tile([P, 2, 512], U32, name="xq%d" % g, align_bytes=64) for g in range(2)]
+        xs = [const.tile([P, 2, 512], U8, name="xs%d" % g, align_bytes=64) for g in range(2)]
+        ys = [const.tile([P, 2, WID[k]], U8, name="ys%d" % k, align_bytes=64) for k in range(NK - 2)]
+        ys_end = const.tile([P, 2, F - OFF[-2]], U8, name="ys_end", align_bytes=64)
+        h_span = [[const.tile([P, 4, sum(WID[k] for k in ks)], BF16, name="h%d%d" % (s, g)) for g in range(2)] for s, ks in enumerate(SPANS)]
 
         ctx.enter_context(tc.manual_schedule())
 
-        h_t, m_t, th_t, pen_t, g_t, gq_t, gs_t = {}, {}, {}, {}, {}, {}, {}
-        up_t, y32_t, yil_t, yb_t = {}, {}, {}, {}
+        th_t, pen_t, g_t, gq_t, gs_t = {}, {}, {}, {}, {}
+        up_t, y32_t, yil_t, yb_t, yq_t = {}, {}, {}, {}, {}
         r_raw, x_raw, rg_t, rb_t = {}, {}, {}, {}
 
-        def load_h(u):
+        def load_h(s, g):
+            lo = OFF[SPANS[s][0]]
+            hi = lo + sum(WID[k] for k in SPANS[s])
+            nc.sync.dma_start(out=h_span[s][g][:], in_=h[512 * g : 512 * g + 512, lo:hi].rearrange("(p t) f -> p t f", t=4))
+
+        def h_view(u):
             k, g = divmod(u, 2)
-            h_t[u] = hpool.tile([P, 4, WID[k]], BF16, name="h_in")
-            src = h[512 * g : 512 * g + 512, OFF[k] : OFF[k] + WID[k]].rearrange("(p t) f -> p t f", t=4)
-            nc.sync.dma_start(out=h_t[u][:], in_=src)
+            s = SPAN_OF[k]
+            lo = OFF[k] - OFF[SPANS[s][0]]
+            return h_span[s][g][:, :, lo : lo + WID[k]]
 
         def load_rows(dst, src, g, lo=0, hi=4):
             if lo == 0:
@@ -106,24 +114,31 @@ def tile_transcodertanhpenaltyencodervjp_x2_kernel(tc, x, h, r, wdec_words, wdec
                 nc.scalar.copy(out=out, in_=in_)
 
         def r_copy(g, c, tp, engine):
-            if tp == 0:
-                rg_t[(g, c)] = ilpool.tile([P, 2048], BF16, name="grouped", align_bytes=64)
-            dst = rg_t[(g, c)][:].bitcast(F32)[:, 512 * tp : 512 * (tp + 1)].rearrange("p (t m e) -> p t m e", t=2, e=2)
+            if tp == 0 and c == 0:
+                rg_t[g] = ilpool.tile([P, 4096], BF16, name="grouped", align_bytes=64)
+            lo = 1024 * c + 512 * tp
+            dst = rg_t[g][:].bitcast(F32)[:, lo : lo + 512].rearrange("p (t m e) -> p t m e", t=2, e=2)
             copy(engine, dst, rb_t[(g, c, tp)][:].rearrange("p (t e m) -> p t m e", t=2, e=2))
 
-        def r_quant(g, c):
-            nc.vector.quantize_mx(out=rq[g][c][:].bitcast(E4M3), scales=rs[g][c][:], in_=rg_t[(g, c)][:])
+        def r_quant(g, lo, hi):
+            nc.vector.quantize_mx(
+                out=rq[g][:, lo:hi, :].rearrange("p c n -> p (c n)").bitcast(E4M3),
+                scales=rs[g][:, lo:hi, :].rearrange("p c n -> p (c n)"),
+                in_=rg_t[g][:, 2048 * lo : 2048 * hi],
+            )
 
         def x_copy(g, half, engine):
             if engine == "-":
                 return
-            xg = ilpool.tile([P, 2048], BF16, name="grouped", align_bytes=64)
-            rg_t[("x", g, half)] = xg
-            dst = xg[:].rearrange("p (t m j) -> p t m j", t=4, j=4)
+            if half == 0:
+                rg_t[("x", g)] = ilpool.tile([P, 4096], BF16, name="grouped", align_bytes=64)
+            dst = rg_t[("x", g)][:, 2048 * half : 2048 * half + 2048].rearrange("p (t m j) -> p t m j", t=4, j=4)
             copy(engine, dst, x_raw[g][:, :, 512 * half : 512 * half + 512].rearrange("p j (m t) -> p t m j", t=4))
 
-        def x_quant(g, half):
-            nc.vector.quantize_mx(out=xq[g][half][:].bitcast(E4M3), scales=xs[g][half][:], in_=rg_t[("x", g, half)][:])
+        def x_quant(g):
+            nc.vector.quantize_mx(
+                out=xq[g][:].rearrange("p c n -> p (c n)").bitcast(E4M3), scales=xs[g][:].rearrange("p c n -> p (c n)"), in_=rg_t[("x", g)][:]
+            )
 
         lam_bank = {}
 
@@ -136,16 +151,15 @@ def tile_transcodertanhpenaltyencodervjp_x2_kernel(tc, x, h, r, wdec_words, wdec
 
         def tanh(u):
             th_t[u] = thpool.tile([P, 4, WID[u // 2]], F32, name="th")
-            nc.scalar.activation(out=th_t[u][:], in_=h_t[u][:], func=ACT.Tanh)
+            nc.scalar.activation(out=th_t[u][:], in_=h_view(u), func=ACT.Tanh)
 
         def square(u):
             nc.scalar.activation(out=th_t[u][:], in_=th_t[u][:], func=ACT.Square)
 
-        def mask(u):
-            k, g = divmod(u, 2)
-            m_t[u] = mpool.tile([P, 4, WID[k]], BF16, name="mask")
+        def mask(s, g):
             for t in range(4):
-                nc.vector.tensor_scalar(out=m_t[u][:, t, :], in0=h_t[u][:, t, :], scalar1=0.0, scalar2=w_col[:, g, t : t + 1], op0=ALU.is_gt, op1=ALU.mult)
+                row = h_span[s][g][:, t, :]
+                nc.vector.tensor_scalar(out=row, in0=row, scalar1=0.0, scalar2=w_col[:, g, t : t + 1], op0=ALU.is_gt, op1=ALU.mult)
 
         def step_a(u):
             n = WID[u // 2]
@@ -164,8 +178,8 @@ def tile_transcodertanhpenaltyencodervjp_x2_kernel(tc, x, h, r, wdec_words, wdec
                     for c in range(2):
                         nc.tensor.matmul_mx(
                             out=bank[:, lo : lo + n],
-                            lhsT=rq[g][c][:, P * t : P * t + P].bitcast(E4M3),
-                            lhsT_scale=rs[g][c][:, P * t : P * t + P],
+                            lhsT=rq[g][:, c, P * t : P * t + P].bitcast(E4M3),
+                            lhsT_scale=rs[g][:, c, P * t : P * t + P],
                             rhs=w_words[k][:, c, 2 * lo : 2 * (lo + n)].bitcast(E2M1),
                             rhs_scale=w_scales[:, c, OFF[k] + lo : OFF[k] + lo + n],
                             start=(c == 0),
@@ -180,8 +194,8 @@ def tile_transcodertanhpenaltyencodervjp_x2_kernel(tc, x, h, r, wdec_words, wdec
             if hi <= lo:
                 return
             if u not in g_t:
-                g_t[u] = ilpool.tile([P, 4 * WID[u // 2]], BF16, name="grouped", align_bytes=64)
-            dst, a, b = g_t[u][:, 4 * lo : 4 * hi], pen_t[u][:, :, lo:hi], m_t[u][:, :, lo:hi]
+                g_t[u] = gpool.tile([P, 4 * WID[u // 2]], BF16, name="g_in", align_bytes=64)
+            dst, a, b = g_t[u][:, 4 * lo : 4 * hi], pen_t[u][:, :, lo:hi], h_view(u)[:, :, lo:hi]
             if engine == "v":
                 nc.vector.tensor_tensor(
                     out=dst.rearrange("p (c i t) -> p c t i", i=4, t=4),
@@ -210,8 +224,8 @@ def tile_transcodertanhpenaltyencodervjp_x2_kernel(tc, x, h, r, wdec_words, wdec
                     u = 2 * k + g
                     nc.tensor.matmul_mx(
                         out=bank[:, 0 : WID[k]],
-                        lhsT=xq[g][half][:, P * t : P * t + P].bitcast(E4M3),
-                        lhsT_scale=xs[g][half][:, P * t : P * t + P],
+                        lhsT=xq[g][:, half, P * t : P * t + P].bitcast(E4M3),
+                        lhsT_scale=xs[g][:, half, P * t : P * t + P],
                         rhs=gq_t[u][:].bitcast(E4M3),
                         rhs_scale=gs_t[u][:],
                         start=(g == 0),
@@ -235,47 +249,59 @@ def tile_transcodertanhpenaltyencodervjp_x2_kernel(tc, x, h, r, wdec_words, wdec
         def y_group(k, half, lo, hi, engine):
             if hi <= lo:
                 return
-            if (k, half) not in yil_t:
-                yil_t[(k, half)] = ilpool.tile([P, 4 * WID[k]], BF16, name="grouped", align_bytes=64)
-            dst = yil_t[(k, half)][:, 4 * lo : 4 * hi].rearrange("p (c i t) -> p c t i", i=4, t=4)
+            if k not in yil_t:
+                yil_t[k] = ilpool.tile([P, 8 * WID[k]], BF16, name="grouped", align_bytes=64)
+            base = 4 * WID[k] * half
+            dst = yil_t[k][:, base + 4 * lo : base + 4 * hi].rearrange("p (c i t) -> p c t i", i=4, t=4)
             copy(engine, dst, y32_t[(k, half)][:, :, lo:hi].rearrange("p t (c i) -> p c t i", i=4))
 
-        def y_quant(k, half):
-            yq = gqpool.tile([P, WID[k]], U32, name="yq", align_bytes=64)
-            cols = slice(OFF[k], OFF[k] + WID[k])
-            i = max(0, k - NK + 3)
-            lo = OFF[k] - ys_cols[i][0]
-            nc.vector.quantize_mx(out=yq[:].bitcast(E4M3), scales=ys[i][:, half, lo : lo + WID[k]], in_=yil_t[(k, half)][:])
-            nc.sync.dma_start(out=out_1[half, :, cols, :].rearrange("p m t -> p (m t)").bitcast(I32), in_=yq[:].bitcast(I32))
+        def y_quant(k, lo, hi):
+            n = WID[k]
+            if k not in yq_t:
+                yq_t[k] = gqpool.tile([P, 2, n], U32, name="yq", align_bytes=64)
+            yq = yq_t[k]
+            nc.vector.quantize_mx(
+                out=yq[:, lo:hi, :].rearrange("p c n -> p (c n)").bitcast(E4M3),
+                scales=ys[k][:, lo:hi, :].rearrange("p c n -> p (c n)") if k < NK - 2 else ys_end[:, lo, OFF[k] - OFF[-2] : OFF[k] - OFF[-2] + n],
+                in_=yil_t[k][:, 4 * n * lo : 4 * n * hi],
+            )
 
-        def y_scales(i):
-            lo, hi = ys_cols[i]
-            for q in range(4):
+        def y_codes(k, lo, hi):
+            dst = out_1[lo:hi, :, OFF[k] : OFF[k] + WID[k], :].rearrange("c p m t -> p c (m t)").bitcast(I32)
+            nc.sync.dma_start(out=dst, in_=yq_t[k][:, lo:hi, :].bitcast(I32))
+
+        def y_scales(tile, lo, hi):
+            for e in range(4):
                 nc.sync.dma_start(
-                    out=out_2[:, 4 * q : 4 * q + 4, lo:hi].rearrange("c q n -> q c n").bitcast(I32), in_=ys[i][32 * q : 32 * q + 4, :, :].bitcast(I32)
+                    out=out_2[:, 4 * e : 4 * e + 4, lo:hi].rearrange("c q n -> q c n").bitcast(I32), in_=tile[32 * e : 32 * e + 4, :, :].bitcast(I32)
                 )
 
         make_identity(nc, ident[:])
         nc.gpsimd.memset(w_scales[:].rearrange("p c n -> p (c n)").bitcast(I32), 0)
         nc.vector.memset(lam_rows[:], 0.0)
-        load_h(0)
+        load_h(0, 0)
         load_rows(r_raw, r, 0, 0, 2)
         nc.sync.dma_start(out=w_raw[:], in_=w.rearrange("(g p t) -> p g t", p=P, t=4))
         nc.sync.dma_start(out=lam_rows[0:16, :], in_=lam.rearrange("(k p) -> k p", p=P))
         load_rows(r_raw, r, 0, 2, 4)
-        load_h(1)
+        load_h(0, 1)
         load_words(0)
         load_w_scales()
-        load_rows(r_raw, r, 1)
-        load_h(2)
-        load_rows(x_raw, x, 0)
-        load_h(3)
-        load_rows(x_raw, x, 1)
-        load_words(1)
-        for u in range(4, UNITS):
-            load_h(u)
-            if u % 2 == 1:
-                load_words(u // 2)
+        for item in "raxby":
+            if item == "r":
+                load_rows(r_raw, r, 1)
+            elif item == "a":
+                load_h(1, 0)
+            elif item == "b":
+                load_h(1, 1)
+            elif item == "x":
+                load_rows(x_raw, x, 0)
+            else:
+                load_rows(x_raw, x, 1)
+        for k in range(1, NK):
+            load_words(k)
+            if k < 3:
+                load_h(2, k - 1)
 
         tanh(0)
         square(0)
@@ -283,39 +309,39 @@ def tile_transcodertanhpenaltyencodervjp_x2_kernel(tc, x, h, r, wdec_words, wdec
         nc.vector.tensor_copy(out=w_col[:], in_=w_raw[:])
         r_copy(0, 0, 0, "v")
         nc.vector.tensor_copy(out=lam_f32[:], in_=lam_rows[:])
-        r_copy(0, 1, 0, "s")
-        r_copy(0, 0, 1, "v")
-        r_copy(0, 1, 1, "v")
+        r_copy(0, 1, 0, "svs"[0])
+        r_copy(0, 0, 1, "svs"[1])
+        r_copy(0, 1, 1, "svs"[2])
         tanh(1)
         square(1)
         lamT = lam_ps.tile([P, 512], F32, name="lam_bank")
         nc.tensor.transpose(lamT[:, 0:P], lam_f32[:], ident[:])
-        r_quant(0, 0)
-        r_quant(0, 1)
+        r_quant(0, 0, 1)
+        r_quant(0, 1, 2)
         nc.vector.tensor_scalar(out=lam_cols[:], in0=lamT[:, 0:16], scalar1=-1.0, scalar2=None, op0=ALU.mult)
         lam_transposes(0)
         stage1(0)
-        mask(0)
+        mask(0, 0)
         r_transposes(1, y_ps, "yb")
         step_a(0)
-        tanh(2)
+        if 0 == 0:
+            tanh(2)
 
         for u in range(UNITS):
             last = u == UNITS - 1
             ku, hu = divmod(u - 3, 2)
+            if u + 1 < UNITS:
+                step_a(u + 1)
+            step_b(u)
             if u == 0:
-                step_a(1)
-                step_b(0)
-                r_copy(1, 0, 0, "v")
-                r_copy(1, 1, 0, "v")
-                r_copy(1, 0, 1, "v")
-                r_copy(1, 1, 1, "v")
-                r_quant(1, 0)
-                r_quant(1, 1)
-            else:
-                if u + 1 < UNITS:
-                    step_a(u + 1)
-                step_b(u)
+                r_copy(1, 0, 0, "vvvv"[0])
+                r_copy(1, 1, 0, "vvvv"[1])
+                r_copy(1, 0, 1, "vvvv"[2])
+                r_copy(1, 1, 1, "vvvv"[3])
+                mask(0, 1)
+                r_quant(1, 0, 2)
+            if u == 0 and 0 == 1:
+                tanh(2)
             if u + 1 < UNITS:
                 stage1(u + 1)
             if u % 2 == 0 and u + 2 < UNITS:
@@ -323,56 +349,56 @@ def tile_transcodertanhpenaltyencodervjp_x2_kernel(tc, x, h, r, wdec_words, wdec
             if u + 2 < UNITS:
                 square(u + 2)
             if u >= 3:
-                y_out(ku, hu, 0, "s")
-                y_out(ku, hu, 1, "s")
+                for t in range(4):
+                    if YO[u - 3][t] == "v":
+                        y_out(ku, hu, t, "v")
+                y_out(ku, hu, 0, "s") if YO[u - 3][0] == "s" else None
+                y_out(ku, hu, 1, "s") if YO[u - 3][1] == "s" else None
+                y_store(ku, hu, 0, 2)
             if u + 3 < UNITS:
                 tanh(u + 3)
             if u >= 3:
-                y_out(ku, hu, 2, "s")
-                y_out(ku, hu, 3, "s")
-                y_store(ku, hu)
+                y_out(ku, hu, 2, "s") if YO[u - 3][2] == "s" else None
+                y_out(ku, hu, 3, "s") if YO[u - 3][3] == "s" else None
+                y_store(ku, hu, 2, 4)
             if u < 2:
                 x_copy(u, 0, "vvvs"[2 * u])
                 x_copy(u, 1, "vvvs"[2 * u + 1])
+                x_quant(u)
             if u >= 1:
                 step_c(u - 1, CG[u - 1], WID[(u - 1) // 2], "v")
-            if u < 2:
-                x_quant(u, 0)
-                x_quant(u, 1)
-            if u >= 1:
-                g_quant(u - 1)
-            if last:
-                break
-            if u >= 4:
-                kp, hp = divmod(u - 4, 2)
-                y_quant(kp, hp)
+            if u >= 5 and u % 2 == 1 and not last:
+                y_quant((u - 5) // 2, 0, 2)
+                y_codes((u - 5) // 2, 0, 2)
+                y_scales(ys[(u - 5) // 2], OFF[(u - 5) // 2], OFF[(u - 3) // 2])
+            if u in {2: (1, 0), 3: (1, 1), 6: (2, 0), 7: (2, 1)}:
+                mask(*{2: (1, 0), 3: (1, 1), 6: (2, 0), 7: (2, 1)}[u])
             if u >= 3:
                 y_group(ku, hu, 0, VC[u - 3], "v")
-                y_group(ku, hu, VC[u - 3], WID[ku], "s")
+                if not last:
+                    y_group(ku, hu, VC[u - 3], WID[ku], "s")
+            if u >= 1:
+                g_quant(u - 1)
             if u >= 2:
                 k2, h2 = divmod(u - 2, 2)
                 stage2(k2, h2, y_ps, "yb")
-            if u >= 1:
-                mask(u)
-            if u == UNITS - 2:
-                mask(u + 1)
-            step_c(u, 0, CG[u], "g")
+            if not last:
+                step_c(u, 0, CG[u], "g")
 
         z = NK - 1
         n = WID[z]
         m = 160
         step_c(UNITS - 1, 0, n, "v")
-        y_quant(z - 2, 1)
-        y_scales(0)
+        y_quant(z - 2, 0, 2)
         g_quant(UNITS - 1)
-        y_group(z - 1, 0, 0, VC[UNITS - 4], "v")
-        y_group(z - 1, 0, VC[UNITS - 4], WID[z - 1], "s")
-        stage2(z - 1, 1, y_ps, "yb")
         for t in range(4):
             y_out(z - 1, 1, t, "s")
-        y_store(z - 1, 1)
+            if t % 2 == 1:
+                y_store(z - 1, 1, t - 1, t + 1)
+        y_codes(z - 2, 0, 2)
+        y_scales(ys[z - 2], OFF[z - 2], OFF[z - 1])
+        y_group(z - 1, 0, VC[UNITS - 4], WID[z - 1], "s")
         stage2(z, 0, up_ps, "up")
-        y_quant(z - 1, 0)
         stage2(z, 1, y_ps, "yb")
         for t in range(4):
             y_out(z, 0, t, "v" if t < 3 else "s")
@@ -380,16 +406,19 @@ def tile_transcodertanhpenaltyencodervjp_x2_kernel(tc, x, h, r, wdec_words, wdec
         y_group(z - 1, 1, 0, VC[UNITS - 3], "v")
         y_group(z - 1, 1, VC[UNITS - 3], WID[z - 1], "s")
         y_group(z, 0, 0, m, "v")
-        y_quant(z - 1, 1)
-        y_scales(1)
+        y_quant(z - 1, 0, 1)
+        y_quant(z - 1, 1, 2)
+        y_codes(z - 1, 0, 2)
         y_group(z, 0, m, n, "s")
         y_out(z, 1, 0, "v")
         y_out(z, 1, 1, "s")
-        y_quant(z, 0)
         y_out(z, 1, 2, "s")
+        y_quant(z, 0, 1)
         y_out(z, 1, 3, "v")
         y_store(z, 1)
+        y_codes(z, 0, 1)
         y_group(z, 1, m, n, "s")
         y_group(z, 1, 0, m, "v")
-        y_quant(z, 1)
-        y_scales(2)
+        y_quant(z, 1, 2)
+        y_codes(z, 1, 2)
+        y_scales(ys_end, OFF[-2], F)

from contextlib import ExitStack

import concourse.mybir as mybir
from concourse.masks import make_identity

T, D, F = 1024, 1024, 2048
FLOPS = 2 * (2 * T * D * F)
BYTES = 2 * (T * D + T * F + T * D + F + T) + D * F // 2 + D * F // 32 + 4 * D * F + D * F + D * F // 32

P = 128
WID = [256,512,512,512,256]
OFF = [sum(WID[:i]) for i in range(len(WID))]
NK = len(WID)
SPANS = [[0],[1,2],[3,4]]
SPAN_OF = {k: s for s, ks in enumerate(SPANS) for k in ks}
YO = ["ssss","ssss","ssss","ssss","ssss","ssss","ssss","ssss","ssss","ssss"]
GI = 4
UNITS = 2 * NK
CG = [256,256,448,448,448,448,384,256,0,0]
VC = [0,0,0,0,0,0,128,256]

F32 = mybir.dt.float32
BF16 = mybir.dt.bfloat16
U32 = mybir.dt.uint32
I32 = mybir.dt.int32
U8 = mybir.dt.uint8
E4M3 = mybir.dt.float8_e4m3fn_x4
E2M1 = mybir.dt.float4_e2m1fn_x4
ALU = mybir.AluOpType
ACT = mybir.ActivationFunctionType


def tile_transcodertanhpenaltyencodervjp_x2_kernel(tc, x, h, r, wdec_words, wdec_scales, lam, w, out_0, out_1, out_2):
    nc = tc.nc
    with ExitStack() as ctx:
        const = ctx.enter_context(tc.tile_pool(name="const", bufs=1))
        raws = ctx.enter_context(tc.tile_pool(name="raws", bufs=3))
        thpool = ctx.enter_context(tc.tile_pool(name="thpool", bufs=4))
        penpool = ctx.enter_context(tc.tile_pool(name="penpool", bufs=3))
        ilpool = ctx.enter_context(tc.tile_pool(name="ilpool", bufs=3))
        gpool = ctx.enter_context(tc.tile_pool(name="gpool", bufs=1))
        gqpool = ctx.enter_context(tc.tile_pool(name="gqpool", bufs=4))
        ypool = ctx.enter_context(tc.tile_pool(name="ypool", bufs=3))
        up_ps = ctx.enter_context(tc.psum_pool(name="up_ps", bufs=4))
        y_ps = ctx.enter_context(tc.psum_pool(name="y_ps", bufs=3))
        lam_ps = ctx.enter_context(tc.psum_pool(name="lam_ps", bufs=1))

        ident = const.tile([P, P], F32, name="ident")
        w_raw = const.tile([P, 2, 4], BF16, name="w_raw")
        w_col = const.tile([P, 2, 4], F32, name="w_col")
        lam_rows = const.tile([P, P], BF16, name="lam_rows")
        lam_f32 = const.tile([P, P], F32, name="lam_f32")
        lam_cols = const.tile([P, 16], F32, name="lam_cols")
        w_words = [const.tile([P, 2, 2 * WID[k]], U8, name="w_words%d" % k, align_bytes=64) for k in range(NK)]
        w_scales = const.tile([P, 2, F], U8, name="w_scales", align_bytes=64)
        rq = [const.tile([P, 2, 512], U32, name="rq%d" % g, align_bytes=64) for g in range(2)]
        rs = [const.tile([P, 2, 512], U8, name="rs%d" % g, align_bytes=64) for g in range(2)]
        xq = [const.tile([P, 2, 512], U32, name="xq%d" % g, align_bytes=64) for g in range(2)]
        xs = [const.tile([P, 2, 512], U8, name="xs%d" % g, align_bytes=64) for g in range(2)]
        ys = [const.tile([P, 2, WID[k]], U8, name="ys%d" % k, align_bytes=64) for k in range(NK - 2)]
        ys_end = const.tile([P, 2, F - OFF[-2]], U8, name="ys_end", align_bytes=64)
        h_span = [[const.tile([P, 4, sum(WID[k] for k in ks)], BF16, name="h%d%d" % (s, g)) for g in range(2)] for s, ks in enumerate(SPANS)]

        ctx.enter_context(tc.manual_schedule())

        th_t, pen_t, g_t, gq_t, gs_t = {}, {}, {}, {}, {}
        up_t, y32_t, yil_t, yb_t, yq_t = {}, {}, {}, {}, {}
        r_raw, x_raw, rg_t, rb_t = {}, {}, {}, {}

        def load_h(s, g):
            lo = OFF[SPANS[s][0]]
            hi = lo + sum(WID[k] for k in SPANS[s])
            nc.sync.dma_start(out=h_span[s][g][:], in_=h[512 * g : 512 * g + 512, lo:hi].rearrange("(p t) f -> p t f", t=4))

        def h_view(u):
            k, g = divmod(u, 2)
            s = SPAN_OF[k]
            lo = OFF[k] - OFF[SPANS[s][0]]
            return h_span[s][g][:, :, lo : lo + WID[k]]

        def load_rows(dst, src, g, lo=0, hi=4):
            if lo == 0:
                dst[g] = raws.tile([P, 4, D], BF16, name="raw")
            rows = src[512 * g : 512 * g + 512, :].rearrange("(p t) d -> p t d", t=4)
            nc.sync.dma_start(out=dst[g][:, lo:hi, :], in_=rows[:, lo:hi, :])

        def load_words(k):
            cols = slice(2 * OFF[k], 2 * (OFF[k] + WID[k]))
            nc.sync.dma_start(out=w_words[k][:].bitcast(I32), in_=wdec_words[:, :, cols].rearrange("c p b -> p c b").bitcast(I32))

        def load_w_scales():
            for q in range(4):
                nc.sync.dma_start(
                    out=w_scales[32 * q : 32 * q + 4, :, :].bitcast(I32), in_=wdec_scales[:, 4 * q : 4 * q + 4, :].rearrange("c q n -> q c n").bitcast(I32)
                )

        def r_transposes(g, pool, nm):
            for tp in range(2):
                for c in range(2):
                    bank = pool.tile([P, 512], F32, name=nm)
                    rb_t[(g, c, tp)] = bank
                    for t in range(2):
                        words = r_raw[g][:, 2 * tp + t, :].bitcast(F32)
                        for e in range(2):
                            o = (2 * t + e) * P
                            nc.tensor.transpose(bank[:, o : o + P], words[:, 256 * c + e : 256 * (c + 1) : 2], ident[:])

        def copy(engine, out, in_):
            if engine == "v":
                nc.vector.tensor_copy(out=out, in_=in_)
            elif engine == "g":
                nc.gpsimd.tensor_scalar(out=out, in0=in_, scalar1=1.0, scalar2=1.0, op0=ALU.mult, op1=ALU.mult)
            else:
                nc.scalar.copy(out=out, in_=in_)

        def r_copy(g, c, tp, engine):
            if tp == 0 and c == 0:
                rg_t[g] = ilpool.tile([P, 4096], BF16, name="grouped", align_bytes=64)
            lo = 1024 * c + 512 * tp
            dst = rg_t[g][:].bitcast(F32)[:, lo : lo + 512].rearrange("p (t m e) -> p t m e", t=2, e=2)
            copy(engine, dst, rb_t[(g, c, tp)][:].rearrange("p (t e m) -> p t m e", t=2, e=2))

        def r_quant(g, lo, hi):
            nc.vector.quantize_mx(
                out=rq[g][:, lo:hi, :].rearrange("p c n -> p (c n)").bitcast(E4M3),
                scales=rs[g][:, lo:hi, :].rearrange("p c n -> p (c n)"),
                in_=rg_t[g][:, 2048 * lo : 2048 * hi],
            )

        def x_copy(g, half, engine):
            if engine == "-":
                return
            if half == 0:
                rg_t[("x", g)] = ilpool.tile([P, 4096], BF16, name="grouped", align_bytes=64)
            dst = rg_t[("x", g)][:, 2048 * half : 2048 * half + 2048].rearrange("p (t m j) -> p t m j", t=4, j=4)
            copy(engine, dst, x_raw[g][:, :, 512 * half : 512 * half + 512].rearrange("p j (m t) -> p t m j", t=4))

        def x_quant(g):
            nc.vector.quantize_mx(
                out=xq[g][:].rearrange("p c n -> p (c n)").bitcast(E4M3), scales=xs[g][:].rearrange("p c n -> p (c n)"), in_=rg_t[("x", g)][:]
            )

        lam_bank = {}

        def lam_transposes(k):
            bank = lam_ps.tile([P, 512], F32, name="lam_bank")
            lam_bank[k] = bank
            for b in range(WID[k] // P):
                col = OFF[k] // P + b
                nc.tensor.transpose(bank[:, P * b : P * b + P], lam_cols[:, col : col + 1].to_broadcast([P, P]), ident[:])

        def tanh(u):
            th_t[u] = thpool.tile([P, 4, WID[u // 2]], F32, name="th")
            nc.scalar.activation(out=th_t[u][:], in_=h_view(u), func=ACT.Tanh)

        def square(u):
            nc.scalar.activation(out=th_t[u][:], in_=th_t[u][:], func=ACT.Square)

        def mask(s, g):
            for t in range(4):
                row = h_span[s][g][:, t, :]
                nc.vector.tensor_scalar(out=row, in0=row, scalar1=0.0, scalar2=w_col[:, g, t : t + 1], op0=ALU.is_gt, op1=ALU.mult)

        def step_a(u):
            n = WID[u // 2]
            pen_t[u] = penpool.tile([P, 4, n], F32, name="pen")
            nc.vector.scalar_tensor_tensor(
                out=pen_t[u][:], in0=th_t[u][:], scalar=1.0, in1=lam_bank[u // 2][:, 0:n].unsqueeze(1).to_broadcast([P, 4, n]), op0=ALU.subtract, op1=ALU.mult
            )

        def stage1(u):
            k, g = divmod(u, 2)
            n = 512 if WID[k] == 512 else 128
            for t in range(4):
                bank = up_ps.tile([P, 512], F32, name="up")
                up_t[(u, t)] = bank
                for lo in range(0, WID[k], n):
                    for c in range(2):
                        nc.tensor.matmul_mx(
                            out=bank[:, lo : lo + n],
                            lhsT=rq[g][:, c, P * t : P * t + P].bitcast(E4M3),
                            lhsT_scale=rs[g][:, c, P * t : P * t + P],
                            rhs=w_words[k][:, c, 2 * lo : 2 * (lo + n)].bitcast(E2M1),
                            rhs_scale=w_scales[:, c, OFF[k] + lo : OFF[k] + lo + n],
                            start=(c == 0),
                            stop=(c == 1),
                        )

        def step_b(u):
            for t in range(4):
                nc.vector.tensor_tensor(out=pen_t[u][:, t, :], in0=pen_t[u][:, t, :], in1=up_t[(u, t)][:, 0 : WID[u // 2]], op=ALU.add)

        def step_c(u, lo, hi, engine):
            if hi <= lo:
                return
            if u not in g_t:
                g_t[u] = gpool.tile([P, 4 * WID[u // 2]], BF16, name="g_in", align_bytes=64)
            dst, a, b = g_t[u][:, 4 * lo : 4 * hi], pen_t[u][:, :, lo:hi], h_view(u)[:, :, lo:hi]
            if engine == "v":
                nc.vector.tensor_tensor(
                    out=dst.rearrange("p (c i t) -> p c t i", i=4, t=4),
                    in0=a.rearrange("p t (c i) -> p c t i", i=4),
                    in1=b.rearrange("p t (c i) -> p c t i", i=4),
                    op=ALU.mult,
                )
            else:
                nc.gpsimd.tensor_tensor(
                    out=dst.rearrange("p (c i t) -> p c t i", i=GI, t=4),
                    in0=a.rearrange("p t (c i) -> p c t i", i=GI),
                    in1=b.rearrange("p t (c i) -> p c t i", i=GI),
                    op=ALU.mult,
                )

        def g_quant(u):
            gq_t[u] = gqpool.tile([P, WID[u // 2]], U32, name="gq", align_bytes=64)
            gs_t[u] = gqpool.tile([P, WID[u // 2]], U8, name="gs", align_bytes=64)
            nc.vector.quantize_mx(out=gq_t[u][:].bitcast(E4M3), scales=gs_t[u][:], in_=g_t[u][:])

        def stage2(k, half, pool, nm):
            for t in range(4):
                bank = pool.tile([P, 512], F32, name=nm)
                yb_t[(k, half, t)] = bank
                for g in range(2):
                    u = 2 * k + g
                    nc.tensor.matmul_mx(
                        out=bank[:, 0 : WID[k]],
                        lhsT=xq[g][:, half, P * t : P * t + P].bitcast(E4M3),
                        lhsT_scale=xs[g][:, half, P * t : P * t + P],
                        rhs=gq_t[u][:].bitcast(E4M3),
                        rhs_scale=gs_t[u][:],
                        start=(g == 0),
                        stop=(g == 1),
                    )

        def y_out(k, half, t, engine):
            if t == 0:
                y32_t[(k, half)] = ypool.tile([P, 4, WID[k]], F32, name="y32")
            dst = y32_t[(k, half)][:, t, :]
            src = yb_t[(k, half, t)][:, 0 : WID[k]]
            if engine == "v":
                nc.vector.tensor_scalar(out=dst, in0=src, scalar1=0.03125, scalar2=None, op0=ALU.mult)
            else:
                nc.scalar.activation(out=dst, in_=src, func=ACT.Copy, scale=0.03125)

        def y_store(k, half, lo=0, hi=4):
            dst = out_0[512 * half : 512 * half + 512, OFF[k] : OFF[k] + WID[k]].rearrange("(p t) m -> p t m", t=4)
            nc.sync.dma_start(out=dst[:, lo:hi, :], in_=y32_t[(k, half)][:, lo:hi, :])

        def y_group(k, half, lo, hi, engine):
            if hi <= lo:
                return
            if k not in yil_t:
                yil_t[k] = ilpool.tile([P, 8 * WID[k]], BF16, name="grouped", align_bytes=64)
            base = 4 * WID[k] * half
            dst = yil_t[k][:, base + 4 * lo : base + 4 * hi].rearrange("p (c i t) -> p c t i", i=4, t=4)
            copy(engine, dst, y32_t[(k, half)][:, :, lo:hi].rearrange("p t (c i) -> p c t i", i=4))

        def y_quant(k, lo, hi):
            n = WID[k]
            if k not in yq_t:
                yq_t[k] = gqpool.tile([P, 2, n], U32, name="yq", align_bytes=64)
            yq = yq_t[k]
            nc.vector.quantize_mx(
                out=yq[:, lo:hi, :].rearrange("p c n -> p (c n)").bitcast(E4M3),
                scales=ys[k][:, lo:hi, :].rearrange("p c n -> p (c n)") if k < NK - 2 else ys_end[:, lo, OFF[k] - OFF[-2] : OFF[k] - OFF[-2] + n],
                in_=yil_t[k][:, 4 * n * lo : 4 * n * hi],
            )

        def y_codes(k, lo, hi):
            dst = out_1[lo:hi, :, OFF[k] : OFF[k] + WID[k], :].rearrange("c p m t -> p c (m t)").bitcast(I32)
            nc.sync.dma_start(out=dst, in_=yq_t[k][:, lo:hi, :].bitcast(I32))

        def y_scales(tile, lo, hi):
            for e in range(4):
                nc.sync.dma_start(
                    out=out_2[:, 4 * e : 4 * e + 4, lo:hi].rearrange("c q n -> q c n").bitcast(I32), in_=tile[32 * e : 32 * e + 4, :, :].bitcast(I32)
                )

        make_identity(nc, ident[:])
        nc.gpsimd.memset(w_scales[:].rearrange("p c n -> p (c n)").bitcast(I32), 0)
        nc.vector.memset(lam_rows[:], 0.0)
        load_h(0, 0)
        load_rows(r_raw, r, 0, 0, 2)
        nc.sync.dma_start(out=w_raw[:], in_=w.rearrange("(g p t) -> p g t", p=P, t=4))
        nc.sync.dma_start(out=lam_rows[0:16, :], in_=lam.rearrange("(k p) -> k p", p=P))
        load_rows(r_raw, r, 0, 2, 4)
        load_h(0, 1)
        load_words(0)
        load_w_scales()
        for item in "raxby":
            if item == "r":
                load_rows(r_raw, r, 1)
            elif item == "a":
                load_h(1, 0)
            elif item == "b":
                load_h(1, 1)
            elif item == "x":
                load_rows(x_raw, x, 0)
            else:
                load_rows(x_raw, x, 1)
        for k in range(1, NK):
            load_words(k)
            if k < 3:
                load_h(2, k - 1)

        tanh(0)
        square(0)
        r_transposes(0, up_ps, "up")
        nc.vector.tensor_copy(out=w_col[:], in_=w_raw[:])
        r_copy(0, 0, 0, "v")
        nc.vector.tensor_copy(out=lam_f32[:], in_=lam_rows[:])
        r_copy(0, 1, 0, "svs"[0])
        r_copy(0, 0, 1, "svs"[1])
        r_copy(0, 1, 1, "svs"[2])
        tanh(1)
        square(1)
        lamT = lam_ps.tile([P, 512], F32, name="lam_bank")
        nc.tensor.transpose(lamT[:, 0:P], lam_f32[:], ident[:])
        r_quant(0, 0, 1)
        r_quant(0, 1, 2)
        nc.vector.tensor_scalar(out=lam_cols[:], in0=lamT[:, 0:16], scalar1=-1.0, scalar2=None, op0=ALU.mult)
        lam_transposes(0)
        stage1(0)
        mask(0, 0)
        r_transposes(1, y_ps, "yb")
        step_a(0)
        if 0 == 0:
            tanh(2)

        for u in range(UNITS):
            last = u == UNITS - 1
            ku, hu = divmod(u - 3, 2)
            if u + 1 < UNITS:
                step_a(u + 1)
            step_b(u)
            if u == 0:
                r_copy(1, 0, 0, "vvvv"[0])
                r_copy(1, 1, 0, "vvvv"[1])
                r_copy(1, 0, 1, "vvvv"[2])
                r_copy(1, 1, 1, "vvvv"[3])
                mask(0, 1)
                r_quant(1, 0, 2)
            if u == 0 and 0 == 1:
                tanh(2)
            if u + 1 < UNITS:
                stage1(u + 1)
            if u % 2 == 0 and u + 2 < UNITS:
                lam_transposes(u // 2 + 1)
            if u + 2 < UNITS:
                square(u + 2)
            if u >= 3:
                for t in range(4):
                    if YO[u - 3][t] == "v":
                        y_out(ku, hu, t, "v")
                y_out(ku, hu, 0, "s") if YO[u - 3][0] == "s" else None
                y_out(ku, hu, 1, "s") if YO[u - 3][1] == "s" else None
                y_store(ku, hu, 0, 2)
            if u + 3 < UNITS:
                tanh(u + 3)
            if u >= 3:
                y_out(ku, hu, 2, "s") if YO[u - 3][2] == "s" else None
                y_out(ku, hu, 3, "s") if YO[u - 3][3] == "s" else None
                y_store(ku, hu, 2, 4)
            if u < 2:
                x_copy(u, 0, "vvvs"[2 * u])
                x_copy(u, 1, "vvvs"[2 * u + 1])
                x_quant(u)
            if u >= 1:
                step_c(u - 1, CG[u - 1], WID[(u - 1) // 2], "v")
            if u >= 5 and u % 2 == 1 and not last:
                y_quant((u - 5) // 2, 0, 2)
                y_codes((u - 5) // 2, 0, 2)
                y_scales(ys[(u - 5) // 2], OFF[(u - 5) // 2], OFF[(u - 3) // 2])
            if u in {2: (1, 0), 3: (1, 1), 6: (2, 0), 7: (2, 1)}:
                mask(*{2: (1, 0), 3: (1, 1), 6: (2, 0), 7: (2, 1)}[u])
            if u >= 3:
                y_group(ku, hu, 0, VC[u - 3], "v")
                if not last:
                    y_group(ku, hu, VC[u - 3], WID[ku], "s")
            if u >= 1:
                g_quant(u - 1)
            if u >= 2:
                k2, h2 = divmod(u - 2, 2)
                stage2(k2, h2, y_ps, "yb")
            if not last:
                step_c(u, 0, CG[u], "g")

        z = NK - 1
        n = WID[z]
        m = 160
        step_c(UNITS - 1, 0, n, "v")
        y_quant(z - 2, 0, 2)
        g_quant(UNITS - 1)
        for t in range(4):
            y_out(z - 1, 1, t, "s")
            if t % 2 == 1:
                y_store(z - 1, 1, t - 1, t + 1)
        y_codes(z - 2, 0, 2)
        y_scales(ys[z - 2], OFF[z - 2], OFF[z - 1])
        y_group(z - 1, 0, VC[UNITS - 4], WID[z - 1], "s")
        stage2(z, 0, up_ps, "up")
        stage2(z, 1, y_ps, "yb")
        for t in range(4):
            y_out(z, 0, t, "v" if t < 3 else "s")
        y_store(z, 0)
        y_group(z - 1, 1, 0, VC[UNITS - 3], "v")
        y_group(z - 1, 1, VC[UNITS - 3], WID[z - 1], "s")
        y_group(z, 0, 0, m, "v")
        y_quant(z - 1, 0, 1)
        y_quant(z - 1, 1, 2)
        y_codes(z - 1, 0, 2)
        y_group(z, 0, m, n, "s")
        y_out(z, 1, 0, "v")
        y_out(z, 1, 1, "s")
        y_out(z, 1, 2, "s")
        y_quant(z, 0, 1)
        y_out(z, 1, 3, "v")
        y_store(z, 1)
        y_codes(z, 0, 1)
        y_group(z, 1, m, n, "s")
        y_group(z, 1, 0, m, "v")
        y_quant(z, 1, 2)
        y_codes(z, 1, 2)
        y_scales(ys_end, OFF[-2], F)
